import numpy as np
import ml_dtypes


def mxq(x, axis, fmt="e4m3"):
    dtype, down = {"e4m3": (ml_dtypes.float8_e4m3fn, 7), "e5m2": (ml_dtypes.float8_e5m2, 14)}[fmt]
    v = np.moveaxis(np.asarray(x, np.float32).astype(ml_dtypes.bfloat16).astype(np.float64), axis, -1)
    blocks = v.reshape(v.shape[:-1] + (-1, 32))
    amax = np.abs(blocks).max(-1, keepdims=True)
    byte = np.maximum(np.where(amax > 0, np.frexp(amax)[1] - 1 + 127, 0) - down, 1)
    scale = np.exp2(byte - 127.0)
    codes = (blocks / scale).astype(np.float32).astype(dtype).astype(np.float64)
    return np.moveaxis((codes * scale).reshape(v.shape), -1, axis)


WIDE = False


def mx_kscale(k):
    if not WIDE:
        return np.ones(k)
    levels = np.array([10, -10, 5, -5, 0])
    if k % 512:
        return np.exp2(np.random.permutation(np.resize(levels, k // 32))).repeat(32)
    a = np.empty((k // 512, 16))
    for p in range(k // 512):
        a[p, :8] = np.random.permutation(np.resize(levels, 8))
        for g in range(8):
            far = levels[np.abs(levels - a[p, g]) >= 10]
            a[p, g + 8] = far[np.random.randint(len(far))]
    return np.exp2(a.ravel()).repeat(32)


def f64(x):
    return np.asarray(x).astype(np.float64)


def striped(idx):
    return np.tile(np.asarray(idx).reshape(-1, 16).T, (8, 1)).astype(np.uint16)


def unstriped(offs):
    return offs[:16].T.reshape(-1).astype(np.int64)


E2M1 = np.array([0.0, 0.5, 1.0, 1.5, 2.0, 3.0, 4.0, 6.0, -0.0, -0.5, -1.0, -1.5, -2.0, -3.0, -4.0, -6.0])


def pack_weight(w, fmt):
    k, n = w.shape
    w = f64(np.asarray(w, np.float32).astype(ml_dtypes.bfloat16)).reshape(k // 32, 32, n)
    amax = np.abs(w).max(1)
    if fmt == "e4m3":
        byte = np.frexp(amax)[1] - 1 + 127 - 7
    else:
        mant, ex = np.frexp(amax / 6.0)
        byte = np.where(mant > 0.5, ex, ex - 1) + 127
    byte = np.clip(np.where(amax > 0, byte, 1), 1, 254)
    scaled = (w * np.exp2(127.0 - byte)[:, None, :]).reshape(k, n).astype(np.float32)
    by_word = np.ascontiguousarray(scaled.reshape(k // 512, 128, 4, n).transpose(0, 1, 3, 2))
    if fmt == "e4m3":
        words = by_word.astype(ml_dtypes.float8_e4m3fn).view(np.uint8)
    else:
        c = by_word.astype(ml_dtypes.float4_e2m1fn).view(np.uint8) & 0xF
        words = (c[..., 0::2] | (c[..., 1::2] << 4)).reshape(k // 512, 128, 2 * n)
    return np.ascontiguousarray(words), np.ascontiguousarray(byte.astype(np.uint8).reshape(k // 512, 16, n))


def unpack_weight(words, scales, fmt):
    g, _, n = scales.shape
    words = np.ascontiguousarray(words).reshape(g, 128, n, -1)
    if fmt == "e4m3":
        vals = words.view(ml_dtypes.float8_e4m3fn).astype(np.float64)
    else:
        nib = np.empty((g, 128, n, 4), np.uint8)
        nib[..., 0::2] = words & 0xF
        nib[..., 1::2] = words >> 4
        vals = E2M1[nib]
    vals = vals * np.repeat(np.exp2(scales.astype(np.float64) - 127.0), 8, axis=1)[..., None]
    return vals.transpose(0, 1, 3, 2).reshape(g * 512, n)


D, T, I, Q, E, Z, X = 512, 2048, 512, 128, 512, 1024, 1024


def setup_inputs():
    n = np.random.standard_normal
    idx = np.random.permutation(T)[:I]
    idx2 = np.random.permutation(Z)[:I]
    idx3 = np.random.permutation(X)[:I]
    fd = mx_kscale(D)
    fi = mx_kscale(I)
    ti = np.ones(T)
    ti[idx] = fi
    ti3 = np.ones(X)
    ti3[idx3] = fi
    keysp = pack_weight(n((D, T)) / fd[:, None], "e4m3")
    return {
        "query": (n((D, Q)) * 1.0 / np.sqrt(D) * fd[:, None]).astype(np.float32),
        "keys_words": keysp[0],
        "keys_scales": keysp[1],
        "earl": (np.random.uniform(0.3, 1.7, (Q, Z))).astype(np.float32),
        "os": (np.random.uniform(0.02, 0.08, (1, I)) * fi).astype(np.float32),
        "os2": (np.random.uniform(0.02, 0.08, (1, I)) * fi).astype(np.float32),
        "vals": (n((E, T)) / ti).astype(np.float32),
        "vals2": (n((E, X)) / ti3).astype(np.float32),
        "offs": striped(idx),
        "offs2": striped(idx2),
        "offs3": striped(idx3),
    }


def reference(query, keys_words, keys_scales, earl, os, os2, vals, vals2, offs, offs2, offs3):
    idx = unstriped(offs)
    idx2 = unstriped(offs2)
    idx3 = unstriped(offs3)
    keysu = unpack_weight(keys_words, keys_scales, "e4m3")
    queryq = mxq(f64(query), 0, "e4m3")
    keysidxg = keysu[:, idx]
    a = queryq.T @ keysidxg
    w = a * f64(earl)[:, idx2]
    wo1 = w * f64(os)
    wt1 = wo1.T
    wo2 = w * f64(os2)
    wt2 = wo2.T
    vt1 = f64(vals)[:, idx].T
    vt2 = f64(vals2)[:, idx3].T
    wt1q = mxq(wt1, 0, "e4m3")
    vt1q = mxq(vt1, 0, "e4m3")
    wt2q = mxq(wt2, 0, "e4m3")
    vt2q = mxq(vt2, 0, "e4m3")
    o = wt1q.T @ vt1q + wt2q.T @ vt2q
    return o

@@ -1,0 +1,157 @@
+from contextlib import ExitStack
+
+import concourse.mybir as mybir
+from concourse.masks import make_identity
+
+F32 = mybir.dt.float32
+BF16 = mybir.dt.bfloat16
+I32 = mybir.dt.int32
+U32 = mybir.dt.uint32
+U16 = mybir.dt.uint16
+U8 = mybir.dt.uint8
+FP8X4 = mybir.dt.float8_e4m3fn_x4
+MULT = mybir.AluOpType.mult
+COPY = mybir.ActivationFunctionType.Copy
+
+P = 128
+PACK = 4
+BANK = 512
+D, T, I, Q, E, Z, X = 512, 2048, 512, 128, 512, 1024, 1024
+BLOCKS = E // P
+LIST_COLS = I // 16
+VECTOR_COLS = 12
+
+FLOPS = 2 * Q * I * D + 2 * 2 * Q * I * E
+
+
+def tile_attend_earliertable_twostores_lean_kernel(
+    tc, query, keys_words, keys_scales, earl, factor1, factor2, vals, vals2, offs, offs2, offs3, out
+):
+    nc = tc.nc
+    with ExitStack() as ctx:
+        keep = ctx.enter_context(tc.tile_pool(name="keep", bufs=1))
+        psum = ctx.enter_context(tc.psum_pool(name="psum", bufs=1))
+
+        def sb(shape, dtype, name):
+            return keep.tile(shape, dtype, name=name, align_bytes=64)
+
+        def rows(b):
+            return slice(b * P, (b + 1) * P)
+
+        list1 = sb([P, LIST_COLS], U16, "list1")
+        list2 = sb([P, LIST_COLS], U16, "list2")
+        list3 = sb([P, LIST_COLS], U16, "list3")
+        pool1 = [sb([P, T], F32, f"pool1_{b}") for b in range(BLOCKS)]
+        pool2 = [sb([P, X], F32, f"pool2_{b}") for b in range(BLOCKS)]
+        key_words = sb([P, T], U32, "key_words")
+        key_bytes = sb([P, T], U8, "key_bytes")
+        query_raw = sb([P, PACK, Q], F32, "query_raw")
+        earl_pool = sb([P, Z], F32, "earl_pool")
+        slot_factor = [sb([P, PACK], F32, f"slot_factor{s}") for s in range(2)]
+        ident = sb([P, P], F32, "ident")
+        banks = [psum.tile([P, BANK], F32, name=f"bank{j}") for j in range(2)]
+
+        nc.gpsimd.memset(key_bytes[:].bitcast(I32), 0)
+        make_identity(nc, ident[:])
+
+        nc.sync.dma_start(query_raw[:], query.rearrange("(p t) q -> p t q", t=PACK))
+        for quad in range(4):
+            nc.sync.dma_start(
+                out=key_bytes[32 * quad : 32 * quad + 4, :].bitcast(I32),
+                in_=keys_scales[0, 4 * quad : 4 * quad + 4, :].bitcast(I32),
+            )
+        nc.sync.dma_start(list1[:], offs)
+        nc.sync.dma_start(list2[:], offs2)
+        nc.sync.dma_start(earl_pool[:], earl)
+        nc.sync.dma_start(key_words[:].bitcast(I32), keys_words[0].rearrange("p n t -> p (n t)").bitcast(I32))
+        for s, factor in enumerate((factor1, factor2)):
+            nc.sync.dma_start(out=slot_factor[s][:], in_=factor.rearrange("o (p t) -> (o p) t", t=PACK))
+        nc.sync.dma_start(list3[:], offs3)
+        for half in range(2):
+            for b in (2 * half, 2 * half + 1):
+                nc.sync.dma_start(pool2[b][:], vals2[rows(b), :])
+            for b in (2 * half, 2 * half + 1):
+                nc.sync.dma_start(pool1[b][:], vals[rows(b), :])
+
+        def planes(width, name):
+            return sb([P, width], U32, name + "_codes"), sb([P, width], U8, name + "_scales")
+
+        def quantise(dst, cols, grouped):
+            nc.vector.quantize_mx(out=dst[0][:, cols].bitcast(FP8X4), scales=dst[1][:, cols], in_=grouped)
+
+        def product(acc, lhs, rhs, cols, start, stop):
+            nc.tensor.matmul_mx(
+                out=acc,
+                lhsT=lhs[0][:].bitcast(FP8X4),
+                lhsT_scale=lhs[1][:],
+                rhs=rhs[0][:, cols].bitcast(FP8X4),
+                rhs_scale=rhs[1][:, cols],
+                start=start,
+                stop=stop,
+            )
+
+        def gather_values(picked, pool, offsets, vector_cols):
+            cut = 16 * vector_cols
+            if vector_cols > 0:
+                nc.vector.tensor_copy(out=picked[:, :cut], in_=pool[:].indirect(offsets[:, :vector_cols]))
+            nc.scalar.activation(out=picked[:, cut:], in_=pool[:].indirect(offsets[:, vector_cols:]), func=COPY)
+
+        def turn_values(picked, bank, dst, b, name):
+            words = picked[:].bitcast(F32)
+            for u in range(2):
+                nc.tensor.transpose(bank[:, rows(u)], words[:, u::2], ident[:])
+            grouped = sb([P, P * PACK], BF16, name)
+            nc.vector.tensor_copy(
+                out=grouped[:].bitcast(F32).rearrange("p (e u) -> p e u", u=2),
+                in_=bank[:, : 2 * P].rearrange("p (u e) -> p e u", u=2),
+            )
+            quantise(dst, rows(b), grouped[:])
+
+        values1 = planes(E, "values1")
+        values2 = planes(E, "values2")
+        picked2 = [sb([P, I], BF16, f"picked2_{b}") for b in range(BLOCKS)]
+        picked1 = [sb([P, I], BF16, f"picked1_{b}") for b in range(BLOCKS)]
+
+        query_grouped = sb([P, Q * PACK], BF16, "query_grouped")
+        nc.vector.tensor_copy(
+            out=query_grouped[:].rearrange("p (q t) -> p q t", t=PACK), in_=query_raw[:].rearrange("p t q -> p q t")
+        )
+        keys = planes(I, "keys")
+        nc.vector.tensor_copy(out=keys[1][:], in_=key_bytes[:].indirect(list1[:]))
+        queries = planes(Q, "queries")
+        quantise(queries, slice(0, Q), query_grouped[:])
+        picked_earl = sb([P, I], F32, "picked_earl")
+        nc.scalar.activation(out=picked_earl[:], in_=earl_pool[:].indirect(list2[:]), func=COPY)
+        nc.vector.tensor_copy(out=keys[0][:], in_=key_words[:].indirect(list1[:]))
+        product(banks[0][:], queries, keys, slice(0, I), True, True)
+
+        weights = sb([P, I], F32, "weights")
+        nc.vector.tensor_tensor(out=weights[:], in0=banks[0][:], in1=picked_earl[:], op=MULT)
+        for t in range(PACK):
+            nc.tensor.transpose(banks[1][:, rows(t)], weights[:, t::PACK], ident[:])
+        scaled = [sb([P, Q * PACK], BF16, f"scaled{s}") for s in range(2)]
+        for s in range(2):
+            nc.vector.tensor_tensor(
+                out=scaled[s][:].rearrange("p (q t) -> p q t", t=PACK),
+                in0=banks[1][:].rearrange("p (t q) -> p q t", t=PACK),
+                in1=slot_factor[s][:].unsqueeze(1).to_broadcast([P, Q, PACK]),
+                op=MULT,
+            )
+        weights_mx = [planes(Q, f"weights{s}") for s in range(2)]
+        for s in range(2):
+            quantise(weights_mx[s], slice(0, Q), scaled[s][:])
+
+        for half in range(2):
+            cols = slice(2 * half * P, 2 * (half + 1) * P)
+            for b in (2 * half, 2 * half + 1):
+                gather_values(picked2[b], pool2[b], list3, 0)
+                turn_values(picked2[b], banks[b % 2], values2, b, f"grouped2_{b}")
+            acc = psum.tile([P, 2 * P], F32, name=f"acc{half}")
+            product(acc[:], weights_mx[1], values2, cols, True, False)
+            for b in (2 * half, 2 * half + 1):
+                gather_values(picked1[b], pool1[b], list1, VECTOR_COLS if b == BLOCKS - 1 else 0)
+                turn_values(picked1[b], banks[b % 2], values1, b, f"grouped1_{b}")
+            product(acc[:], weights_mx[0], values1, cols, False, True)
+            result = sb([P, 2 * P], F32, f"result{half}")
+            nc.vector.tensor_copy(out=result[:], in_=acc[:])
+            nc.sync.dma_start(out=out[:, cols], in_=result[:])

@@ -19,7 +19,7 @@ BANK = 512
 D, T, I, Q, E, Z, X = 512, 2048, 512, 128, 512, 1024, 1024
 BLOCKS = E // P
 LIST_COLS = I // 16
-VECTOR_COLS = 12
+VECTOR_COLS = 16
 
 FLOPS = 2 * Q * I * D + 2 * 2 * Q * I * E
 
@@ -55,15 +55,12 @@ def tile_attend_earliertable_twostores_lean_kernel(
         make_identity(nc, ident[:])
 
         nc.sync.dma_start(query_raw[:], query.rearrange("(p t) q -> p t q", t=PACK))
-        for quad in range(4):
-            nc.sync.dma_start(
-                out=key_bytes[32 * quad : 32 * quad + 4, :].bitcast(I32),
-                in_=keys_scales[0, 4 * quad : 4 * quad + 4, :].bitcast(I32),
-            )
+        for r in range(4):
+            nc.sync.dma_start(out=key_bytes[r:P:32, :].bitcast(I32), in_=keys_scales[0, r:16:4, :].bitcast(I32))
         nc.sync.dma_start(list1[:], offs)
+        nc.sync.dma_start(key_words[:].bitcast(I32), keys_words[0].rearrange("p n t -> p (n t)").bitcast(I32))
         nc.sync.dma_start(list2[:], offs2)
         nc.sync.dma_start(earl_pool[:], earl)
-        nc.sync.dma_start(key_words[:].bitcast(I32), keys_words[0].rearrange("p n t -> p (n t)").bitcast(I32))
         for s, factor in enumerate((factor1, factor2)):
             nc.sync.dma_start(out=slot_factor[s][:], in_=factor.rearrange("o (p t) -> (o p) t", t=PACK))
         nc.sync.dma_start(list3[:], offs3)
@@ -96,16 +93,14 @@ def tile_attend_earliertable_twostores_lean_kernel(
                 nc.vector.tensor_copy(out=picked[:, :cut], in_=pool[:].indirect(offsets[:, :vector_cols]))
             nc.scalar.activation(out=picked[:, cut:], in_=pool[:].indirect(offsets[:, vector_cols:]), func=COPY)
 
-        def turn_values(picked, bank, dst, b, name):
+        def turn_values(picked, bank, grouped):
             words = picked[:].bitcast(F32)
             for u in range(2):
                 nc.tensor.transpose(bank[:, rows(u)], words[:, u::2], ident[:])
-            grouped = sb([P, P * PACK], BF16, name)
             nc.vector.tensor_copy(
-                out=grouped[:].bitcast(F32).rearrange("p (e u) -> p e u", u=2),
+                out=grouped.bitcast(F32).rearrange("p (e u) -> p e u", u=2),
                 in_=bank[:, : 2 * P].rearrange("p (u e) -> p e u", u=2),
             )
-            quantise(dst, rows(b), grouped[:])
 
         values1 = planes(E, "values1")
         values2 = planes(E, "values2")
@@ -113,8 +108,10 @@ def tile_attend_earliertable_twostores_lean_kernel(
         picked1 = [sb([P, I], BF16, f"picked1_{b}") for b in range(BLOCKS)]
 
         query_grouped = sb([P, Q * PACK], BF16, "query_grouped")
-        nc.vector.tensor_copy(
-            out=query_grouped[:].rearrange("p (q t) -> p q t", t=PACK), in_=query_raw[:].rearrange("p t q -> p q t")
+        nc.scalar.activation(
+            out=query_grouped[:].rearrange("p (q t) -> p q t", t=PACK),
+            in_=query_raw[:].rearrange("p t q -> p q t"),
+            func=COPY,
         )
         keys = planes(I, "keys")
         nc.vector.tensor_copy(out=keys[1][:], in_=key_bytes[:].indirect(list1[:]))
@@ -126,9 +123,14 @@ def tile_attend_earliertable_twostores_lean_kernel(
         product(banks[0][:], queries, keys, slice(0, I), True, True)
 
         weights = sb([P, I], F32, "weights")
-        nc.vector.tensor_tensor(out=weights[:], in0=banks[0][:], in1=picked_earl[:], op=MULT)
+        nc.vector.tensor_tensor(
+            out=weights[:].rearrange("q (t g j) -> q g t j", t=PACK, j=4),
+            in0=banks[0][:].rearrange("q (g j t) -> q g t j", t=PACK, j=4),
+            in1=picked_earl[:].rearrange("q (g j t) -> q g t j", t=PACK, j=4),
+            op=MULT,
+        )
         for t in range(PACK):
-            nc.tensor.transpose(banks[1][:, rows(t)], weights[:, t::PACK], ident[:])
+            nc.tensor.transpose(banks[1][:, rows(t)], weights[:, rows(t)], ident[:])
         scaled = [sb([P, Q * PACK], BF16, f"scaled{s}") for s in range(2)]
         for s in range(2):
             nc.vector.tensor_tensor(
@@ -142,16 +144,16 @@ def tile_attend_earliertable_twostores_lean_kernel(
             quantise(weights_mx[s], slice(0, Q), scaled[s][:])
 
         for half in range(2):
-            cols = slice(2 * half * P, 2 * (half + 1) * P)
-            for b in (2 * half, 2 * half + 1):
-                gather_values(picked2[b], pool2[b], list3, 0)
-                turn_values(picked2[b], banks[b % 2], values2, b, f"grouped2_{b}")
+            pair = (2 * half, 2 * half + 1)
+            cols = slice(pair[0] * P, (pair[1] + 1) * P)
             acc = psum.tile([P, 2 * P], F32, name=f"acc{half}")
-            product(acc[:], weights_mx[1], values2, cols, True, False)
-            for b in (2 * half, 2 * half + 1):
-                gather_values(picked1[b], pool1[b], list1, VECTOR_COLS if b == BLOCKS - 1 else 0)
-                turn_values(picked1[b], banks[b % 2], values1, b, f"grouped1_{b}")
-            product(acc[:], weights_mx[0], values1, cols, False, True)
+            for store, pools, offsets, picked, values in ((1, pool2, list3, picked2, values2), (0, pool1, list1, picked1, values1)):
+                grouped = sb([P, 2, P * PACK], BF16, f"grouped{store}_{half}")
+                for b in pair:
+                    gather_values(picked[b], pools[b], offsets, VECTOR_COLS if (store, b) == (0, BLOCKS - 1) else 0)
+                    turn_values(picked[b], banks[b % 2], grouped[:, b % 2, :])
+                quantise(values, cols, grouped[:].rearrange("p b c -> p (b c)"))
+                product(acc[:], weights_mx[store], values, cols, store == 1, store == 0)
             result = sb([P, 2 * P], F32, f"result{half}")
             nc.vector.tensor_copy(out=result[:], in_=acc[:])
             nc.sync.dma_start(out=out[:, cols], in_=result[:])

@@ -19,7 +19,7 @@ BANK = 512
 D, T, I, Q, E, Z, X = 512, 2048, 512, 128, 512, 1024, 1024
 BLOCKS = E // P
 LIST_COLS = I // 16
-VECTOR_COLS = 16
+VECTOR_COLS = 6
 
 FLOPS = 2 * Q * I * D + 2 * 2 * Q * I * E
 
@@ -143,17 +143,37 @@ def tile_attend_earliertable_twostores_lean_kernel(
         for s in range(2):
             quantise(weights_mx[s], slice(0, Q), scaled[s][:])
 
-        for half in range(2):
-            pair = (2 * half, 2 * half + 1)
-            cols = slice(pair[0] * P, (pair[1] + 1) * P)
-            acc = psum.tile([P, 2 * P], F32, name=f"acc{half}")
-            for store, pools, offsets, picked, values in ((1, pool2, list3, picked2, values2), (0, pool1, list1, picked1, values1)):
-                grouped = sb([P, 2, P * PACK], BF16, f"grouped{store}_{half}")
-                for b in pair:
-                    gather_values(picked[b], pools[b], offsets, VECTOR_COLS if (store, b) == (0, BLOCKS - 1) else 0)
-                    turn_values(picked[b], banks[b % 2], grouped[:, b % 2, :])
-                quantise(values, cols, grouped[:].rearrange("p b c -> p (b c)"))
-                product(acc[:], weights_mx[store], values, cols, store == 1, store == 0)
-            result = sb([P, 2 * P], F32, f"result{half}")
-            nc.vector.tensor_copy(out=result[:], in_=acc[:])
-            nc.sync.dma_start(out=out[:, cols], in_=result[:])
+        def pair_of_blocks(first, picked, pools, offsets, values, name):
+            grouped = sb([P, 2, P * PACK], BF16, name)
+            for b in (first, first + 1):
+                gather_values(picked[b], pools[b], offsets, 0)
+                turn_values(picked[b], banks[b % 2], grouped[:, b % 2, :])
+            quantise(values, slice(first * P, (first + 2) * P), grouped[:].rearrange("p b c -> p (b c)"))
+
+        front = slice(0, 2 * P)
+        acc_front = psum.tile([P, 2 * P], F32, name="acc_front")
+        pair_of_blocks(0, picked2, pool2, list3, values2, "grouped2_front")
+        product(acc_front[:], weights_mx[1], values2, front, True, False)
+        pair_of_blocks(0, picked1, pool1, list1, values1, "grouped1_front")
+        product(acc_front[:], weights_mx[0], values1, front, False, True)
+        result_front = sb([P, 2 * P], F32, "result_front")
+        nc.vector.tensor_copy(out=result_front[:], in_=acc_front[:])
+        nc.sync.dma_start(out=out[:, front], in_=result_front[:])
+
+        pair_of_blocks(2, picked2, pool2, list3, values2, "grouped2_back")
+        acc_back = {}
+        for b in (2, 3):
+            acc_back[b] = psum.tile([P, P], F32, name=f"acc_{b}")
+            product(acc_back[b][:], weights_mx[1], values2, rows(b), True, False)
+        for b in (2, 3):
+            grouped = sb([P, P * PACK], BF16, f"grouped1_{b}")
+            gather_values(picked1[b], pool1[b], list1, VECTOR_COLS if b == 3 else 0)
+            turn_values(picked1[b], banks[b % 2], grouped[:])
+            quantise(values1, rows(b), grouped[:])
+            product(acc_back[b][:], weights_mx[0], values1, rows(b), False, True)
+        result2 = picked1[3][:].bitcast(F32)[:, :P]
+        nc.scalar.copy(out=result2, in_=acc_back[2][:])
+        nc.sync.dma_start(out=out[:, rows(2)], in_=result2)
+        result3 = sb([P, P], F32, "result3")
+        nc.vector.tensor_copy(out=result3[:], in_=acc_back[3][:])
+        nc.sync.dma_start(out=out[:, rows(3)], in_=result3[:])

@@ -19,7 +19,7 @@ BANK = 512
 D, T, I, Q, E, Z, X = 512, 2048, 512, 128, 512, 1024, 1024
 BLOCKS = E // P
 LIST_COLS = I // 16
-VECTOR_COLS = 6
+VECTOR_COLS = 8
 
 FLOPS = 2 * Q * I * D + 2 * 2 * Q * I * E
 
@@ -54,13 +54,13 @@ def tile_attend_earliertable_twostores_lean_kernel(
         nc.gpsimd.memset(key_bytes[:].bitcast(I32), 0)
         make_identity(nc, ident[:])
 
-        nc.sync.dma_start(query_raw[:], query.rearrange("(p t) q -> p t q", t=PACK))
+        nc.sync.dma_start(earl_pool[:], earl)
         for r in range(4):
             nc.sync.dma_start(out=key_bytes[r:P:32, :].bitcast(I32), in_=keys_scales[0, r:16:4, :].bitcast(I32))
+        nc.sync.dma_start(list2[:], offs2)
         nc.sync.dma_start(list1[:], offs)
         nc.sync.dma_start(key_words[:].bitcast(I32), keys_words[0].rearrange("p n t -> p (n t)").bitcast(I32))
-        nc.sync.dma_start(list2[:], offs2)
-        nc.sync.dma_start(earl_pool[:], earl)
+        nc.sync.dma_start(query_raw[:], query.rearrange("(p t) q -> p t q", t=PACK))
         for s, factor in enumerate((factor1, factor2)):
             nc.sync.dma_start(out=slot_factor[s][:], in_=factor.rearrange("o (p t) -> (o p) t", t=PACK))
         nc.sync.dma_start(list3[:], offs3)
@@ -107,19 +107,19 @@ def tile_attend_earliertable_twostores_lean_kernel(
         picked2 = [sb([P, I], BF16, f"picked2_{b}") for b in range(BLOCKS)]
         picked1 = [sb([P, I], BF16, f"picked1_{b}") for b in range(BLOCKS)]
 
+        picked_earl = sb([P, I], F32, "picked_earl")
+        nc.scalar.activation(out=picked_earl[:], in_=earl_pool[:].indirect(list2[:]), func=COPY)
+        keys = planes(I, "keys")
+        nc.vector.tensor_copy(out=keys[1][:], in_=key_bytes[:].indirect(list1[:]))
+        nc.vector.tensor_copy(out=keys[0][:], in_=key_words[:].indirect(list1[:]))
         query_grouped = sb([P, Q * PACK], BF16, "query_grouped")
         nc.scalar.activation(
             out=query_grouped[:].rearrange("p (q t) -> p q t", t=PACK),
             in_=query_raw[:].rearrange("p t q -> p q t"),
             func=COPY,
         )
-        keys = planes(I, "keys")
-        nc.vector.tensor_copy(out=keys[1][:], in_=key_bytes[:].indirect(list1[:]))
         queries = planes(Q, "queries")
         quantise(queries, slice(0, Q), query_grouped[:])
-        picked_earl = sb([P, I], F32, "picked_earl")
-        nc.scalar.activation(out=picked_earl[:], in_=earl_pool[:].indirect(list2[:]), func=COPY)
-        nc.vector.tensor_copy(out=keys[0][:], in_=key_words[:].indirect(list1[:]))
         product(banks[0][:], queries, keys, slice(0, I), True, True)
 
         weights = sb([P, I], F32, "weights")

from contextlib import ExitStack

import concourse.mybir as mybir
from concourse.masks import make_identity

F32 = mybir.dt.float32
BF16 = mybir.dt.bfloat16
I32 = mybir.dt.int32
U32 = mybir.dt.uint32
U16 = mybir.dt.uint16
U8 = mybir.dt.uint8
FP8X4 = mybir.dt.float8_e4m3fn_x4
MULT = mybir.AluOpType.mult
COPY = mybir.ActivationFunctionType.Copy

P = 128
PACK = 4
BANK = 512
D, T, I, Q, E, Z, X = 512, 2048, 512, 128, 512, 1024, 1024
BLOCKS = E // P
LIST_COLS = I // 16
VECTOR_COLS = 8

FLOPS = 2 * Q * I * D + 2 * 2 * Q * I * E


def tile_attend_earliertable_twostores_lean_kernel(
    tc, query, keys_words, keys_scales, earl, factor1, factor2, vals, vals2, offs, offs2, offs3, out
):
    nc = tc.nc
    with ExitStack() as ctx:
        keep = ctx.enter_context(tc.tile_pool(name="keep", bufs=1))
        psum = ctx.enter_context(tc.psum_pool(name="psum", bufs=1))

        def sb(shape, dtype, name):
            return keep.tile(shape, dtype, name=name, align_bytes=64)

        def rows(b):
            return slice(b * P, (b + 1) * P)

        list1 = sb([P, LIST_COLS], U16, "list1")
        list2 = sb([P, LIST_COLS], U16, "list2")
        list3 = sb([P, LIST_COLS], U16, "list3")
        pool1 = [sb([P, T], F32, f"pool1_{b}") for b in range(BLOCKS)]
        pool2 = [sb([P, X], F32, f"pool2_{b}") for b in range(BLOCKS)]
        key_words = sb([P, T], U32, "key_words")
        key_bytes = sb([P, T], U8, "key_bytes")
        query_raw = sb([P, PACK, Q], F32, "query_raw")
        earl_pool = sb([P, Z], F32, "earl_pool")
        slot_factor = [sb([P, PACK], F32, f"slot_factor{s}") for s in range(2)]
        ident = sb([P, P], F32, "ident")
        banks = [psum.tile([P, BANK], F32, name=f"bank{j}") for j in range(2)]

        nc.gpsimd.memset(key_bytes[:].bitcast(I32), 0)
        make_identity(nc, ident[:])

        nc.sync.dma_start(earl_pool[:], earl)
        for r in range(4):
            nc.sync.dma_start(out=key_bytes[r:P:32, :].bitcast(I32), in_=keys_scales[0, r:16:4, :].bitcast(I32))
        nc.sync.dma_start(list2[:], offs2)
        nc.sync.dma_start(list1[:], offs)
        nc.sync.dma_start(key_words[:].bitcast(I32), keys_words[0].rearrange("p n t -> p (n t)").bitcast(I32))
        nc.sync.dma_start(query_raw[:], query.rearrange("(p t) q -> p t q", t=PACK))
        for s, factor in enumerate((factor1, factor2)):
            nc.sync.dma_start(out=slot_factor[s][:], in_=factor.rearrange("o (p t) -> (o p) t", t=PACK))
        nc.sync.dma_start(list3[:], offs3)
        for half in range(2):
            for b in (2 * half, 2 * half + 1):
                nc.sync.dma_start(pool2[b][:], vals2[rows(b), :])
            for b in (2 * half, 2 * half + 1):
                nc.sync.dma_start(pool1[b][:], vals[rows(b), :])

        def planes(width, name):
            return sb([P, width], U32, name + "_codes"), sb([P, width], U8, name + "_scales")

        def quantise(dst, cols, grouped):
            nc.vector.quantize_mx(out=dst[0][:, cols].bitcast(FP8X4), scales=dst[1][:, cols], in_=grouped)

        def product(acc, lhs, rhs, cols, start, stop):
            nc.tensor.matmul_mx(
                out=acc,
                lhsT=lhs[0][:].bitcast(FP8X4),
                lhsT_scale=lhs[1][:],
                rhs=rhs[0][:, cols].bitcast(FP8X4),
                rhs_scale=rhs[1][:, cols],
                start=start,
                stop=stop,
            )

        def gather_values(picked, pool, offsets, vector_cols):
            cut = 16 * vector_cols
            if vector_cols > 0:
                nc.vector.tensor_copy(out=picked[:, :cut], in_=pool[:].indirect(offsets[:, :vector_cols]))
            nc.scalar.activation(out=picked[:, cut:], in_=pool[:].indirect(offsets[:, vector_cols:]), func=COPY)

        def turn_values(picked, bank, grouped):
            words = picked[:].bitcast(F32)
            for u in range(2):
                nc.tensor.transpose(bank[:, rows(u)], words[:, u::2], ident[:])
            nc.vector.tensor_copy(
                out=grouped.bitcast(F32).rearrange("p (e u) -> p e u", u=2),
                in_=bank[:, : 2 * P].rearrange("p (u e) -> p e u", u=2),
            )

        values1 = planes(E, "values1")
        values2 = planes(E, "values2")
        picked2 = [sb([P, I], BF16, f"picked2_{b}") for b in range(BLOCKS)]
        picked1 = [sb([P, I], BF16, f"picked1_{b}") for b in range(BLOCKS)]

        picked_earl = sb([P, I], F32, "picked_earl")
        nc.scalar.activation(out=picked_earl[:], in_=earl_pool[:].indirect(list2[:]), func=COPY)
        keys = planes(I, "keys")
        nc.vector.tensor_copy(out=keys[1][:], in_=key_bytes[:].indirect(list1[:]))
        nc.vector.tensor_copy(out=keys[0][:], in_=key_words[:].indirect(list1[:]))
        query_grouped = sb([P, Q * PACK], BF16, "query_grouped")
        nc.scalar.activation(
            out=query_grouped[:].rearrange("p (q t) -> p q t", t=PACK),
            in_=query_raw[:].rearrange("p t q -> p q t"),
            func=COPY,
        )
        queries = planes(Q, "queries")
        quantise(queries, slice(0, Q), query_grouped[:])
        product(banks[0][:], queries, keys, slice(0, I), True, True)

        weights = sb([P, I], F32, "weights")
        nc.vector.tensor_tensor(
            out=weights[:].rearrange("q (t g j) -> q g t j", t=PACK, j=4),
            in0=banks[0][:].rearrange("q (g j t) -> q g t j", t=PACK, j=4),
            in1=picked_earl[:].rearrange("q (g j t) -> q g t j", t=PACK, j=4),
            op=MULT,
        )
        for t in range(PACK):
            nc.tensor.transpose(banks[1][:, rows(t)], weights[:, rows(t)], ident[:])
        scaled = [sb([P, Q * PACK], BF16, f"scaled{s}") for s in range(2)]
        for s in range(2):
            nc.vector.tensor_tensor(
                out=scaled[s][:].rearrange("p (q t) -> p q t", t=PACK),
                in0=banks[1][:].rearrange("p (t q) -> p q t", t=PACK),
                in1=slot_factor[s][:].unsqueeze(1).to_broadcast([P, Q, PACK]),
                op=MULT,
            )
        weights_mx = [planes(Q, f"weights{s}") for s in range(2)]
        for s in range(2):
            quantise(weights_mx[s], slice(0, Q), scaled[s][:])

        def pair_of_blocks(first, picked, pools, offsets, values, name):
            grouped = sb([P, 2, P * PACK], BF16, name)
            for b in (first, first + 1):
                gather_values(picked[b], pools[b], offsets, 0)
                turn_values(picked[b], banks[b % 2], grouped[:, b % 2, :])
            quantise(values, slice(first * P, (first + 2) * P), grouped[:].rearrange("p b c -> p (b c)"))

        front = slice(0, 2 * P)
        acc_front = psum.tile([P, 2 * P], F32, name="acc_front")
        pair_of_blocks(0, picked2, pool2, list3, values2, "grouped2_front")
        product(acc_front[:], weights_mx[1], values2, front, True, False)
        pair_of_blocks(0, picked1, pool1, list1, values1, "grouped1_front")
        product(acc_front[:], weights_mx[0], values1, front, False, True)
        result_front = sb([P, 2 * P], F32, "result_front")
        nc.vector.tensor_copy(out=result_front[:], in_=acc_front[:])
        nc.sync.dma_start(out=out[:, front], in_=result_front[:])

        pair_of_blocks(2, picked2, pool2, list3, values2, "grouped2_back")
        acc_back = {}
        for b in (2, 3):
            acc_back[b] = psum.tile([P, P], F32, name=f"acc_{b}")
            product(acc_back[b][:], weights_mx[1], values2, rows(b), True, False)
        for b in (2, 3):
            grouped = sb([P, P * PACK], BF16, f"grouped1_{b}")
            gather_values(picked1[b], pool1[b], list1, VECTOR_COLS if b == 3 else 0)
            turn_values(picked1[b], banks[b % 2], grouped[:])
            quantise(values1, rows(b), grouped[:])
            product(acc_back[b][:], weights_mx[0], values1, rows(b), False, True)
        result2 = picked1[3][:].bitcast(F32)[:, :P]
        nc.scalar.copy(out=result2, in_=acc_back[2][:])
        nc.sync.dma_start(out=out[:, rows(2)], in_=result2)
        result3 = sb([P, P], F32, "result3")
        nc.vector.tensor_copy(out=result3[:], in_=acc_back[3][:])
        nc.sync.dma_start(out=out[:, rows(3)], in_=result3[:])
